import numpy as np, ml_dtypes
CORES = [51,54,179,182]
N = 4
BF = ml_dtypes.bfloat16
def gentries(a):
    return np.ascontiguousarray(a.reshape(8, 16, -1).transpose(0, 2, 1)).reshape(8, -1)
def gtable(e):
    e = np.asarray(e); return np.ascontiguousarray(e.reshape(8, -1, 16).transpose(0, 2, 1)).reshape(128, -1).astype(np.int32)
T, C, E, D = 2048, 1024, 64, 8
def ints(rng, *shape):
    return rng.integers(-15, 16, shape).astype(np.float32).astype(BF)
def uneven(rng, *shape):
    s = rng.choice(np.array([0, 1, 3, 7, 15, 15]), shape[:-2] + (1, shape[-1]))
    return ((rng.integers(-15, 16, shape) * s) // 15).astype(np.float32).astype(BF)
def trees(rng, out, alone, tight, across):
    H = T // 2; i = np.arange(T); r = np.arange(N)[:, None, None]
    back = np.where(rng.random((N, 8, T)) < 0.5, rng.integers(1, 9, (N, 8, T)), 1 + np.floor(i * rng.random((N, 8, T))).astype(np.int64))
    pa = np.maximum(i - back, 0)
    pa = np.where(rng.random((N, 8, T)) < alone, i, pa)
    pa = np.where((rng.random((N, 8, T)) < out) & (i >= H) & (r > 0), T + rng.integers(0, E, (N, 8, T)), pa)
    at = rng.integers(0, H, (N, 8, E))
    if tight:
        w = H + np.arange(tight * D).reshape(tight, D)
        pa[:, :, w[:, :-1].reshape(-1)] = w[:, 1:].reshape(-1)
        pa[:, :, w[:, -1]] = np.where(r > 0, T + rng.integers(0, E, (N, 8, tight)), rng.integers(0, H, (N, 8, tight)))
        at[:, :, :tight] = w[:, 0]
    at = rng.permuted(at, axis=2)
    num = rng.permuted(np.tile(i, (N, 8, 1)), axis=2)
    par = np.zeros((N, 8, T), np.int64)
    np.put_along_axis(par, num, np.where(pa < T, np.take_along_axis(num, np.minimum(pa, T - 1), 2), pa), 2)
    ex = np.take_along_axis(np.roll(num, 1, axis=0), at, 2)
    u = np.where(rng.random((N, 8, C)) < 0.75, rng.integers(H, T, (N, 8, C)), rng.integers(0, T, (N, 8, C)))
    up = np.take_along_axis(num, u, 2)
    up = np.where((rng.random((N, 8, C)) < across) & (r > 0), T + rng.integers(0, E, (N, 8, C)), up)
    return up, par, ex
def pack(rng, up, par, ex):
    ex = ex.copy(); ex[0] = rng.integers(0, T, (8, E))
    return {"q": ints(rng, N, 128, C), "k": ints(rng, N, 128, T), "v": ints(rng, N, 128, T), "b": rng.integers(-15, 16, (N, 128, D)).astype(np.float32),
            "up": np.stack([gtable(a) for a in up]), "par": par.astype(np.int32), "ex": np.stack([gtable(a) for a in ex])}
def setup_inputs(rng):
    return pack(rng, *trees(rng, 0.125, 0.015625, E // 4, 0.125))
def setup_inputs_roots(rng):
    up, par, ex = trees(rng, 0.125, 0.5, 0, 0.125)
    par[:, :, 0] = 0; par[:, :, T - 1] = T - 1; par[:, :, 1] = 2; par[:, :, 2] = 3; par[:, :, 3] = 1
    ex[:, :, 0] = 0; ex[:, :, E - 1] = T - 1; ex[:, :, 1] = 1
    up[:, :, 0] = 0; up[:, :, 1] = T - 1; up[:, :, 2] = 1
    up[1:, :, 3] = T; up[1:, :, 4] = T + 1; up[1:, :, C - 1] = T + E - 1; up[0, :, C - 1] = T - 1
    return pack(rng, up, par, ex)
def setup_inputs_brink(rng):
    return pack(rng, *trees(rng, 0.5, 0.015625, E, 0.5))
def setup_inputs_alike(rng):
    up, par, ex = trees(rng, 0.25, 0.015625, 0, 0.0)
    up = np.repeat(up[:, :, :1], C, axis=2); ex = np.repeat(ex[:, :, :1], E, axis=2)
    up[rng.integers(1, N)] = T + rng.integers(0, E, (8, 1))
    return pack(rng, up, par, ex)
def setup_inputs_spread(rng):
    d = setup_inputs(rng)
    d["q"] = uneven(rng, N, 128, C); d["k"] = uneven(rng, N, 128, T); d["v"] = uneven(rng, N, 128, T)
    d["b"] = rng.choice(np.array([-15, -1, 0, 0, 1, 15]), (N, 128, D)).astype(np.float32); return d
def check_inputs(d):
    bad = []
    for n in ("q", "k", "v", "b"):
        w = d[n].astype(np.float32)
        if not ((np.abs(w) <= 15) & (w == np.rint(w))).all(): bad.append(n + ": whole numbers from -15 to 15")
    for n in ("up", "par"):
        w = d[n]
        if w.min() < 0 or w.max() >= T + E or w[0].max() >= T: bad.append(n + ": range")
    if d["ex"].min() < 0 or d["ex"].max() >= T: bad.append("ex: range")
    if bad: return bad
    for r in range(1, N):
        a = gentries(d["ex"][r]).astype(np.int64)
        for t in range(D - 1):
            a = np.take_along_axis(d["par"][r - 1], a, 1).astype(np.int64)
            if (a >= T).any(): return ["the nodes above an exit's node"]
    return bad
def reference(q, k, v, b, up, par, ex):
    y = np.zeros((N, 128, C), np.float32)
    u = np.stack([gentries(a) for a in up]).astype(np.int64); x = np.stack([gentries(a) for a in ex]).astype(np.int64)
    def place(m, r, g):
        return np.where(m < T, r * T + m, (r - 1) * T + x[r, g][np.maximum(m - T, 0)])
    for g in range(8):
        s = slice(16 * g, 16 * g + 16)
        above = np.concatenate([place(par[r, g].astype(np.int64), r, g) for r in range(N)])
        kk = np.concatenate([k[r, s].astype(np.float32) for r in range(N)], axis=1); vv = np.concatenate([v[r, s].astype(np.float32) for r in range(N)], axis=1)
        for r in range(N):
            a = place(u[r, g], r, g); qq = q[r, s].astype(np.float32)
            for t in range(D):
                y[r, s] += np.maximum(qq - kk[:, a] + b[r, s, t:t + 1], np.float32(0)) * vv[:, a]
                a = above[a]
    return {"y": y}

@@ -1,0 +1,311 @@
+from concourse.bass import DstId, RemoteDMATransfer
+from concourse.mybir import AluOpType as A, ActivationFunctionType as F
+
+NT, NC, NE, ND = 2048, 1024, 64, 8
+KW = NT + NE * ND
+W0, W0E = 4112, 6224
+HB = 24576.0
+BF, F32, I32, U16 = "bfloat16", "float32", "int32", "uint16"
+SCRATCH = {n: ("sbuf", [128, w], t) for n, w, t in [
+    ("kw", KW, BF), ("vw", KW, BF), ("qs", NC, BF), ("bs", 8, F32), ("bh", 8, BF), ("wt", W0E, BF),
+    ("pc", 128, I32), ("pf", 128, F32), ("pl", 128, U16), ("dg", 256, BF), ("ci", 256, BF),
+    ("ui", 72, I32), ("uh", 72, I32), ("uu", 72, F32), ("uw", 72, F32), ("xs", 16, U16),
+    ("ls", 4 * 72, U16), ("ln", 8 * 72, U16), ("res", 4 * 1088, BF), ("xk", 512, BF), ("xv", 512, BF),
+    ("pi", 8, I32), ("d8", 8, I32), ("h8", 8, I32), ("l128", 128, F32), ("d128", 128, F32), ("cf", 8, F32), ("be", 8, F32),
+    ("bm", 3 * 144, BF), ("idb", 128, BF), ("idh", 256, "float16"),
+    ("xb", ND * NC, BF), ("rb", ND * NC, BF), ("pb", ND * NC, "float16"), ("ys", NC, F32)]}
+SCRATCH.update({n: ("psum", [128, 512], F32) for n in ["acc0", "acc1", "px0", "px1", "px2", "pl0", "pl1", "pl2"]})
+DMAS = ["l_ex", "l_up", "l_par", "l_b", "l_k", "l_v0", "l_q", "i0", "i1", "d0", "d1", "st0", "st1", "st2"]
+SENDS = [("k", 0, 1), ("v", 0, 1), ("kv", 1, 3), ("kv", 3, 5), ("kv", 5, 8)]
+SEMAPHORES = ["cv", "ca", "cp", "cg", "sent", "r_ex", "r_es"] + ["r_x%d" % i for i in range(len(SENDS))] + DMAS
+
+COST = {"cyc": 0.83e-3 * 1.2, "gat": 1.5, "pe": 0.42e-3 * 1.2, "sync": 0.1, "dma": 1.9, "bw": 300e3, "rem": 2.3, "first": 1.3}
+CFG = {
+    "w1": [("v", 0, 62), ("a", 62, 128)],
+    "s": [34, 34, 34, 0],
+    "xv": ["v0", "k1", "v1"],
+    "items": "00v 01p 10v 11p 20p 21p 30v 31p 40p 41v 50p 51p 60p 70v 71p 61p",
+}
+ORDER = """l_ex l_par l_up l_k l_b l_v0 g_pi g_l g_d8 g_d m_w0 c_i16 c_i128 c_ci0 c_ci1 i0 i1 c_t1 c_t3 c_b0 c_al c_o en x_ex
+c_H c_pf uh d1 c_lo d0 uu c_pl uw c_be c_w0x es x_es us m_w1 m_bm c_h8 c_w c_b3 c_b1 c_b2 f0 f1 f2 f3 un c_bh c_ih c_nh c_id
+r_ex l_q xk0 w11 x_x0 w10 r_es s0a s0v t02 xv0 n02 r_x0 s1a t00 s1v n00 k00 t01 t12 x_x1 k01 t10 xv1 n01 n12 xk1 xv2 t11 xk2
+s2a s2v n10 r00 xv3 r_x1 x_x2 xk3 n11 xv4 r_x2 p00 a01 xk4 t22 n22 r01 x_x3 r_x3 s3a p01 t20 k21 k10 t21 n20 k20 n21 r10 xk6
+xk5 xv6 k11 t30 k30 n30 a20 xv5 xv7 xk7 k41 p10 a11 c01 r30 r20 a21 k40 r11 a40 x_x4 r41 p30 k31 c00 a31 p20 c20 r40 r21 r31
+r_x4 p41 k50 c30 c41 p11 c11 k51 k70 c10 k60 p21 a50 r70 r50 p31 p40 a51 k71 r51 a60 c40 p70 a71 p50 p51 r60 c70 k61 r71 c21
+c50 p60 a61 r61 c60 p71 p610 y0 c31 st0 c51 p611 c71 y10 st1 y11 st2"""
+
+
+def plan(T, rank, n, peers, cost):
+    ops = []
+    serve, asks = rank < n - 1, rank > 0
+    cy, gt = cost["cyc"], cost["gat"]
+
+    def op(name, eng, deps, dur, fn, on=True, lat=0.0, kind="c", nb=0.0):
+        ops.append({"name": name, "eng": eng, "deps": [d for d in deps if d], "dur": dur, "fn": fn, "on": on,
+                    "lat": lat, "kind": kind, "nb": nb / cost["bw"]})
+        return name
+
+    def vt(w, c=1.0):
+        return max(64, w * c) * cy + 0.03
+
+    def gat(w):
+        return 0.06 + w * gt * cy
+
+    def dma(name, eng, deps, out, in_, nb, on=True):
+        return op(name, eng, deps, 0.1, lambda e: e.dma_start(out(), in_()), on, cost["dma"], "dma", nb)
+
+    def ts(name, deps, w, out, in0, s1, s2, o0, o1=None, c=1.0):
+        if o1 is None:
+            return op(name, "v", deps, vt(w, c), lambda e: e.tensor_scalar(out(), in0(), s1(), None, o0))
+        return op(name, "v", deps, vt(w, c), lambda e: e.tensor_scalar(out(), in0(), s1(), s2(), o0, o1))
+
+    def aff(name, deps, w, out, in_, scale, bias):
+        return op(name, "a", deps, 0.065 + max(64, w) * cy,
+                  lambda e: e.activation(out(), in_(), F.Identity, bias=bias(), scale=scale()))
+
+    def k_(x):
+        return lambda: x
+
+    def v_(name, a, b, step=1):
+        return lambda: T[name][:, a:b:step]
+
+    def col(j):
+        return v_("cf", j, j + 1)
+
+    def copy(name, deps, w, out, in_, on=True):
+        return op(name, "v", deps, vt(w), lambda e: e.tensor_copy(out(), in_()), on)
+
+    def gather(name, eng, deps, w, out, win, off, on=True):
+        if eng == "v":
+            return op(name, "v", deps, gat(w), lambda e: e.tensor_copy(out(), win().indirect(off())), on)
+        return op(name, "a", deps, gat(w), lambda e: e.activation(out(), win().indirect(off()), F.Identity), on)
+
+    lw = 68 if serve else 64
+    dma("l_ex", "s", [], v_("ui", 64, 68), lambda: T.ex[:], 20e3, asks)
+    dma("l_par", "a", [], v_("pc", 0, 128), lambda: T.par[:], 64e3)
+    dma("l_up", "s", [], v_("ui", 0, 64), lambda: T.up[:], 32e3)
+    dma("l_k", "a", [], v_("kw", 0, NT), lambda: T.k[:], 512e3)
+    dma("l_b", "s", [], v_("bs", 0, 8), lambda: T.b[:], 20e3)
+    dma("l_v0", "s", [], v_("vw", 0, NT), lambda: T.v[:], 512e3)
+    copy("en", ["l_ex"], 4, v_("xs", 0, 4), v_("ui", 64, 68), asks)
+    for x, dep, land, a, more in (("ex", "en", "ln", 0, cost["first"]), ("es", "es", "ls", 8, 0.0)):
+        op("x_" + x, "g", [dep, "g_d"], 1.0,
+           lambda e, x=x, land=land, a=a: e.remote_dma(T[land][:, 64:68], T.xs[:, a:a + 4], T.sem["r_" + x], T.sem.sent,
+                                                       peers["prev"][1], peers["prev"][0], peers["all"]),
+           asks, cost["rem"] + more - 1.4, kind="rem", nb=100e3)
+        op("r_" + x, "x", ["x_" + x], 0, None, serve, kind="arr")
+    fl = {"allow_small_or_imprecise_dtypes": True}
+    op("g_pi", "g", [], 0.15, lambda e: e.iota(T.pi[:, 0:1], [[0, 1]], 0, 1))
+    op("g_l", "g", [], 0.4, lambda e: e.iota(T.l128[:], [[1, 128]], 0, 0, **fl))
+    op("g_d8", "g", [], 0.15, lambda e: e.iota(T.d8[:], [[-16, 8]], 0, 1))
+    op("g_d", "g", [], 0.4, lambda e: e.iota(T.d128[:], [[1, 128]], 0, -1, **fl))
+    op("m_w0", "v", [], vt(NT, 0.5), lambda e: e.memset(T.wt[:, W0:W0 + NT], 0.0))
+    op("m_w1", "v", [], vt(W0 - NT, 0.5), lambda e: e.memset(T.wt[:, NT:W0], 0.0))
+    op("m_bm", "v", [], vt(432, 0.5), lambda e: e.memset(T.bm[:], 0.0))
+    i16, l128 = v_("pi", 1, 2), v_("l128", 0, 128)
+    ts("c_i16", ["g_pi"], 1, i16, v_("pi", 0, 1), k_(15), None, A.bitwise_and)
+    ts("c_i128", ["c_i16"], 1, col(0), i16, k_(128.0), None, A.mult)
+    aff("c_ci0", ["g_l"], 128, v_("ci", 0, 128), l128, k_(1.0), k_(0.0))
+    aff("c_ci1", ["g_l", "c_i128"], 128, v_("ci", 128, 256), l128, k_(0.0), col(0))
+
+    def row(t):
+        return lambda: T.wt[t:128:16, W0:W0 + NT]
+    dma("i0", "s", ["m_w0", "c_ci0"], row(0), v_("ci", 0, 128), 60e3)
+    dma("i1", "s", ["m_w0", "c_ci1"], row(1), v_("ci", 128, 256), 60e3)
+    ts("c_t1", ["c_i16"], 1, col(4), i16, k_(1.0), k_(1728.0), A.is_equal, A.mult)
+    ts("c_t3", ["c_i16"], 1, col(5), i16, k_(3.0), k_(HB + 1792.0), A.is_equal, A.mult)
+    ts("c_b0", ["c_t1", "c_t3"], 1, col(6), col(4), col(5), k_(128.0), A.add, A.add)
+    ts("c_al", ["c_b0"], 1, col(2), col(6), k_(128.0), None, A.is_equal)
+    ts("c_o", ["c_b0"], 1, col(1), col(6), k_(128.0), k_(128.0), A.is_gt, A.mult)
+    ts("c_w", ["c_al"], 1, col(3), col(2), k_(16.0 - 1.0 / 128), k_(1.0 / 128), A.mult, A.add)
+    aff("c_be", ["c_o", "c_b0", "g_l"], 5, v_("be", 0, 5), v_("l128", 0, 5), col(1), col(6))
+    aff("c_w0x", ["c_be", "c_al"], 64, v_("wt", W0 + NT, W0E), v_("l128", 64, 128), col(2), v_("be", 0, 1))
+    fixed = [aff("f%d" % s, ["m_w1", "c_be", "c_al"], 128, v_("wt", NT + 15 + s, NT + s + 2048, 16), l128, col(2),
+                 v_("be", s + 1, s + 2)) for s in range(4)]
+    h8, d128 = v_("h8", 0, 8), v_("d128", 0, 128)
+    ts("c_h8", ["g_d8"], 8, h8, v_("d8", 0, 8), k_(1), None, A.arith_shift_right)
+    ts("c_b1", ["c_h8", "m_bm"], 8, v_("bm", 15, 143, 16), h8, k_(0.0), None, A.is_equal)
+    ts("c_b2", ["c_h8", "m_bm"], 8, v_("bm", 159, 287, 16), h8, k_(1.0), None, A.is_equal)
+    ts("c_b3", ["c_h8", "m_bm", "c_w"], 8, v_("bm", 303, 431, 16), h8, k_(1.0), col(3), A.is_equal, A.mult)
+    ts("c_id", ["g_d"], 128, v_("idb", 0, 128), d128, k_(0.0), None, A.is_equal)
+    ts("c_ih", ["g_d"], 128, v_("idh", 0, 128), d128, k_(0.0), None, A.is_equal)
+    ts("c_nh", ["g_d"], 128, v_("idh", 128, 256), d128, k_(0.0), k_(-1.0), A.is_equal, A.mult)
+    copy("c_bh", ["l_b"], 8, v_("bh", 0, 8), v_("bs", 0, 8))
+    pc, lo_, hi_ = v_("pc", 0, 128), v_("dg", 0, 128), v_("dg", 128, 256)
+    ts("c_H", ["l_par"], 128, hi_, pc, k_(2047.0), k_(HB - 63.5), A.min, A.add)
+    ts("c_pf", ["l_par"], 128, v_("pf", 0, 128), pc, k_(HB), None, A.add)
+    op("c_lo", "v", ["c_H", "c_pf"], vt(256), lambda e: e.tensor_tensor(lo_(), T.pf[:], hi_(), A.subtract))
+    dma("d1", "a", ["m_w0", "c_H"], row(3), hi_, 60e3)
+    dma("d0", "s", ["m_w0", "c_lo"], row(2), lo_, 60e3)
+    dma("l_q", "s", ["d0"], v_("qs", 0, NC), lambda: T.q[:], 256e3)
+    copy("c_pl", ["l_par"], 128, v_("pl", 0, 128), pc)
+    copy("un", ["l_up"], 64, v_("ln", 0, 64), v_("ui", 0, 64))
+    uw = 68 if asks else 64
+    ts("uh", ["l_up", "l_ex"], 68, v_("uh", 0, uw), v_("ui", 0, uw), k_(7), None, A.arith_shift_right)
+    ts("uu", ["uh"], 68, v_("uu", 0, uw), v_("uh", 0, uw), k_(15.0), k_(-2047.0 / 16), A.min, A.mult)
+    op("uw", "v", ["uu"], vt(136), lambda e: e.tensor_tensor(T.uw[:, 0:uw], T.uu[:, 0:uw], T.ui[:, 0:uw], A.add))
+    op("es", "v", ["uw"], vt(4), lambda e: e.tensor_scalar(T.xs[:, 8:12], T.uw[:, 64:68], 16.0, None, A.mult), asks)
+    ts("us", ["uw"], 64, v_("ls", 0, 64), v_("uw", 0, 64), k_(16.0), None, A.mult)
+    w0 = ["i0", "i1", "d0", "d1", "c_w0x", "c_pl"]
+    w1 = fixed + [gather("w1%d" % i, q, w0, 16 * (b - a), v_("wt", 16 * a, 16 * b), v_("wt", W0, W0E), v_("pl", a, b))
+                  for i, (q, a, b) in enumerate(CFG["w1"])]
+    lists = {0: "un"}
+    last_s, bank_free = ["us", "r_es"], [None, None, None]
+    for j in range(4):
+        c, win, x, y = CFG["s"][j], v_("wt", 0, W0), 1088 * j, 72 * j
+        got = []
+        if c:
+            got.append(gather("s%dv" % j, "v", w1 + last_s, 16 * min(c, 68), v_("res", x, x + 16 * min(c, lw)), win,
+                              v_("ls", y, y + min(c, lw))))
+        if c < 64:
+            got.append(gather("s%da" % j, "a", w1 + last_s, 16 * (68 - c), v_("res", x + 16 * c, x + 16 * lw), win,
+                              v_("ls", y + c, y + lw)))
+        for kind in ([2, 0, 1] if j < 3 else [0]):
+            ps = v_("pl%d" % kind, 0, lw)
+
+            def relay(e, x=x, kind=kind, ps=ps):
+                for i in range(16):
+                    r = e.matmul(ps(), T.bm[:, 144 * kind + 15 - i:144 * kind + 143 - i], T.res[:, x + i:x + 16 * lw:16],
+                                 i == 0, i == 15)
+                return r
+            m = op("t%d%d" % (j, kind), "p", got + ["c_b%d" % (kind + 1), bank_free[kind]], 16 * (68 * cost["pe"] + 0.005), relay)
+            d = 2 * j + 1 + kind
+            out = v_("ls", y + 72, y + 72 + lw) if kind == 2 else v_("ln", 72 * d, 72 * d + lw)
+            bank_free[kind] = ts("n%d%d" % (j, kind), [m], 68, out, ps, k_([0.0, -HB, -HB / 128][kind]), None, A.add)
+            if kind == 2:
+                last_s = [bank_free[kind]]
+            else:
+                lists[d] = bank_free[kind]
+    have = {}
+    loads = {"k": ["l_k"], "v": ["l_v0"]}
+    for i, (which, a, b) in enumerate(SENDS):
+        got = []
+        for d in range(a, b):
+            for x in which:
+                got.append(gather("x%s%d" % (x, d), "v" if "%s%d" % (x, d) in CFG["xv"] else "a",
+                                  ["r_ex" if d == 0 else lists[d]] + loads[x], 64, v_("x" + x, 64 * d, 64 * d + 64),
+                                  v_(x + "w", 0, NT), v_("ln", 72 * d + 64, 72 * d + 68), serve))
+                have[x, d] = have.get((x, d - 1), []) + ["r_x%d" % i]
+
+        def give(e, i=i, which=which, a=a, b=b):
+            dst = DstId(rid=peers["next"][0], pnc=peers["next"][1])
+            masks = peers["half"] if len(which) == 2 else [peers["all"]]
+            return e.remote_dma_fused(
+                [RemoteDMATransfer(dst_ids=[dst], dma_engine_mask=masks[u], remote_sem=T.sem["r_x%d" % i],
+                                   src=T["x" + x][:, 64 * a:64 * b], dst=T[x + "w"][:, NT + 64 * a:NT + 64 * b])
+                 for u, x in enumerate(which)], local_sem=T.sem.sent)
+        op("x_x%d" % i, "g", got, 1.0, give, serve, cost["rem"] - 1.4 + (cost["first"] * 0.5 if i == 0 else 0.0),
+           kind="rem", nb=120e3 * len(which))
+        op("r_x%d" % i, "x", ["x_x%d" % i], 0, None, asks, kind="arr")
+    items = CFG["items"].split()
+    acc, xfree, nx, added = [[], []], [None, None, None], 0, [0, 0]
+    for z, (d, h, way) in enumerate(items):
+        t, d = d + h, int(d)
+        a, w = (0, NC) if h == "w" else (512 * int(h), 512)
+        lo, ww = NC * d + a, (NT + NE * (d + 1) if asks else NT)
+
+        def pick(x, a, w, d=d, ww=ww):
+            return T[x][:, 0:ww].indirect(T.ln[:, 72 * d + a // 16:72 * d + (a + w) // 16])
+        xb, rb, qs = v_("xb", lo, lo + w), v_("rb", lo, lo + w), v_("qs", a, a + w)
+        src = [lists[d], "l_k"] + have["k", d]
+        if way == "v":
+            op("k" + t, "v", src + ["l_q"], gat(w),
+               lambda e, xb=xb, qs=qs, pick=pick, a=a, w=w: e.tensor_tensor(xb(), pick("kw", a, w), qs(), A.subtract))
+            clamped = [ts("r" + t, ["k" + t, "c_bh"], w, rb, xb, v_("bh", d, d + 1), k_(0.0), A.subtract, A.min, c=0.5)]
+        else:
+            op("k" + t, "a", src + ["l_b"], gat(w),
+               lambda e, xb=xb, pick=pick, a=a, w=w, d=d: e.activation(xb(), pick("kw", a, w), F.Identity,
+                                                                       bias=T.bs[:, d:d + 1], scale=-1.0))
+            clamped = []
+            for u in range(a // 512, (a + w) // 512):
+                px, x, tu = v_("px%d" % nx, 0, 512), NC * d + 512 * u, "%d%d" % (d, u)
+
+                def addq(e, px=px, x=x, u=u):
+                    e.matmul(px(), T.idb[:], T.qs[:, 512 * u:512 * u + 512], True, False)
+                    return e.matmul(px(), T.idb[:], T.xb[:, x:x + 512], False, True)
+                op("a" + tu, "p", ["k" + t, "l_q", "c_id", xfree[nx]], 1024 * cost["pe"] + 0.05, addq)
+                xfree[nx] = op("r" + tu, "a", ["a" + tu], 0.065 + 512 * cy,
+                               lambda e, px=px, x=x: e.activation(T.rb[:, x:x + 512], px(), F.Relu))
+                clamped.append(xfree[nx])
+                nx = (nx + 1) % 3
+        vsrc = [lists[d]] + clamped + loads["v"] + have["v", d]
+        neg = int(way == "v")
+
+        def times(name, a, w, d=d, pick=pick, vsrc=vsrc):
+            x = NC * d + a
+            return op(name, "v", vsrc, gat(w),
+                      lambda e: e.tensor_tensor(T.pb[:, x:x + w], pick("vw", a, w), T.rb[:, x:x + w], A.mult))
+        if z < len(items) - 1:
+            times("p" + t, a, w)
+            for u in range(a // 512, (a + w) // 512):
+                def add(e, u=u, x=NC * d + 512 * u, neg=neg):
+                    added[u] += 1
+                    return e.matmul(T["acc%d" % u][:], T.idh[:, 128 * neg:128 * neg + 128], T.pb[:, x:x + 512],
+                                    added[u] == 1, added[u] == ND - u)
+                acc[u].append(op("c%d%d" % (d, u), "p", ["p" + t, "c_nh" if neg else "c_ih"], 512 * cost["pe"] + 0.03, add))
+        else:
+            aff("y0", acc[0], 512, v_("ys", 0, 512), v_("acc0", 0, 512), k_(1.0), k_(0.0))
+            dma("st0", "s", ["y0"], v_("y", 0, 512), v_("ys", 0, 512), 256e3)
+            for u in range(2):
+                x = 512 + 256 * u
+                op("y1%d" % u, "v", [times("p%s%d" % (t, u), x, 256)] + acc[1], vt(256),
+                   lambda e, x=x, d=d, neg=neg: e.tensor_tensor(
+                       T.ys[:, x:x + 256], T.acc1[:, x - 512:x - 256], T.pb[:, NC * d + x:NC * d + x + 256],
+                       A.subtract if neg else A.add))
+                dma("st%d" % (u + 1), "sa"[u], ["y1%d" % u], v_("y", x, x + 256), v_("ys", x, x + 256), 128e3)
+    return ops
+
+
+def rank_program(g, core, T, topo):
+    rank = T.rank_of(core)
+    if rank is None:
+        return
+    n = len(T.cores)
+    near = [T.cores[r] for r in (rank - 1, rank + 1) if 0 <= r < n]
+    eng = [e for e in topo.engines(core, near[0]) if e in topo.engines(core, near[-1])]
+    eng = eng[::len(eng) // 8]
+    peers = {"all": sum(1 << e for e in eng), "half": [sum(1 << e for e in eng[0:4]), sum(1 << e for e in eng[4:8])]}
+    if rank > 0:
+        peers["prev"] = topo.addr(T.cores[rank - 1], core)
+    if rank < n - 1:
+        peers["next"] = topo.addr(T.cores[rank + 1], core)
+    ops = {o["name"]: o for o in plan(T, rank, n, peers, COST) if o["on"]}
+    needed = {d for o in ops.values() for d in o["deps"]}
+    queue = {"v": g.vector, "a": g.scalar, "p": g.tensor, "g": g, "s": g.sync}
+    count = {"v": 0, "a": 0, "p": 0, "g": 0}
+    mark, seen, sent = {}, {q: {} for q in queue}, 0
+    for name in ORDER.split():
+        if name not in ops:
+            continue
+        o = ops[name]
+        if o["kind"] == "arr":
+            mark[name] = (name, len(eng))
+            continue
+        e = queue[o["eng"]]
+        want = {}
+        for d in o["deps"]:
+            if d in mark and not (o["eng"] in "pg" and ops[d]["eng"] == o["eng"]):
+                s, v = mark[d]
+                want[s] = max(want.get(s, 0), v)
+        for s, v in want.items():
+            if seen[o["eng"]].get(s, 0) < v:
+                e.wait_ge(T.sem[s], v)
+                seen[o["eng"]][s] = v
+        r = o["fn"](e)
+        if o["kind"] == "dma":
+            r.then_inc(T.sem[name], 16)
+            mark[name] = (name, 16)
+        elif o["kind"] == "rem":
+            sent += len(eng)
+        elif name in needed:
+            count[o["eng"]] += 1
+            r.then_inc(T.sem["c" + o["eng"]], 1)
+            mark[name] = ("c" + o["eng"], count[o["eng"]])
+    last = {}
+    for s, v in mark.values():
+        last[s] = max(last.get(s, 0), v)
+    if sent:
+        last["sent"] = sent
+    for s, v in last.items():
+        if max(seen[q].get(s, 0) for q in seen) < v:
+            g.wait_ge(T.sem[s], v)

@@ -3,188 +3,158 @@ from concourse.mybir import AluOpType as A, ActivationFunctionType as F
 
 NT, NC, NE, ND = 2048, 1024, 64, 8
 KW = NT + NE * ND
-W0, W0E = 4112, 6224
-HB = 24576.0
+W0, W0E = KW, KW + NT + NE
 BF, F32, I32, U16 = "bfloat16", "float32", "int32", "uint16"
 SCRATCH = {n: ("sbuf", [128, w], t) for n, w, t in [
     ("kw", KW, BF), ("vw", KW, BF), ("qs", NC, BF), ("bs", 8, F32), ("bh", 8, BF), ("wt", W0E, BF),
-    ("pc", 128, I32), ("pf", 128, F32), ("pl", 128, U16), ("dg", 256, BF), ("ci", 256, BF),
-    ("ui", 72, I32), ("uh", 72, I32), ("uu", 72, F32), ("uw", 72, F32), ("xs", 16, U16),
-    ("ls", 4 * 72, U16), ("ln", 8 * 72, U16), ("res", 4 * 1088, BF), ("xk", 512, BF), ("xv", 512, BF),
-    ("pi", 8, I32), ("d8", 8, I32), ("h8", 8, I32), ("l128", 128, F32), ("d128", 128, F32), ("cf", 8, F32), ("be", 8, F32),
-    ("bm", 3 * 144, BF), ("idb", 128, BF), ("idh", 256, "float16"),
+    ("pc", 128, I32), ("pl", 128, U16), ("dg", 256, BF), ("ci", 256, BF),
+    ("ui", 72, I32), ("xs", 8, U16), ("xe", 8, U16), ("l0", 64, U16), ("ln", 7 * 68, U16),
+    ("res", 4 * 1088, BF), ("xk", 512, BF), ("xv", 512, BF),
+    ("pi", 8, I32), ("d8", 8, I32), ("h8", 8, I32), ("l8", 8, F32), ("d128", 128, F32), ("cf", 8, F32), ("be", 8, F32),
+    ("bm", 2 * 144, BF), ("idb", 128, BF), ("idh", 256, "float16"),
     ("xb", ND * NC, BF), ("rb", ND * NC, BF), ("pb", ND * NC, "float16"), ("ys", NC, F32)]}
-SCRATCH.update({n: ("psum", [128, 512], F32) for n in ["acc0", "acc1", "px0", "px1", "px2", "pl0", "pl1", "pl2"]})
-DMAS = ["l_ex", "l_up", "l_par", "l_b", "l_k", "l_v0", "l_q", "i0", "i1", "d0", "d1", "st0", "st1", "st2"]
-SENDS = [("k", 0, 1), ("v", 0, 1), ("kv", 1, 3), ("kv", 3, 5), ("kv", 5, 8)]
-SEMAPHORES = ["cv", "ca", "cp", "cg", "sent", "r_ex", "r_es"] + ["r_x%d" % i for i in range(len(SENDS))] + DMAS
-
-COST = {"cyc": 0.83e-3 * 1.2, "gat": 1.5, "pe": 0.42e-3 * 1.2, "sync": 0.1, "dma": 1.9, "bw": 300e3, "rem": 2.3, "first": 1.3}
+SCRATCH.update({n: ("psum", [128, w], F32) for n, w in [("px0", NC), ("px1", NC), ("acc0", 512), ("acc1", 512), ("pla", 512), ("plb", 512)]})
+ACC = [("acc0", 0, 512), ("acc1", 512, 256), ("plb", 768, 256)]
+DMAS = ["l_ex", "l_up", "l_par", "l_b", "l_k", "l_v", "l_q", "i0", "i1", "d0", "d1", "st0", "st1", "st2"]
 CFG = {
-    "w1": [("v", 0, 62), ("a", 62, 128)],
-    "s": [34, 34, 34, 0],
-    "xv": ["v0", "k1", "v1"],
-    "items": "00v 01p 10v 11p 20p 21p 30v 31p 40p 41v 50p 51p 60p 70v 71p 61p",
+    "sends": [("k", 0, 1), ("k", 1, 2), ("v", 0, 2), ("kv", 2, 4), ("kv", 4, 6), ("kv", 6, 8)],
+    "w1": [("a", 0, 70), ("v", 70, 128)],
+    "s": [36, 34, 34, 14],
+    "xv": ["x", "k1", "k2"],
+    "items": "00v 01p 10v 11p 20v 21p 30v 31p 40v 41p 50p 51p 60p 61p 70p 71p",
 }
-ORDER = """l_ex l_par l_up l_k l_b l_v0 g_pi g_l g_d8 g_d m_w0 c_i16 c_i128 c_ci0 c_ci1 i0 i1 c_t1 c_t3 c_b0 c_al c_o en x_ex
-c_H c_pf uh d1 c_lo d0 uu c_pl uw c_be c_w0x es x_es us m_w1 m_bm c_h8 c_w c_b3 c_b1 c_b2 f0 f1 f2 f3 un c_bh c_ih c_nh c_id
-r_ex l_q xk0 w11 x_x0 w10 r_es s0a s0v t02 xv0 n02 r_x0 s1a t00 s1v n00 k00 t01 t12 x_x1 k01 t10 xv1 n01 n12 xk1 xv2 t11 xk2
-s2a s2v n10 r00 xv3 r_x1 x_x2 xk3 n11 xv4 r_x2 p00 a01 xk4 t22 n22 r01 x_x3 r_x3 s3a p01 t20 k21 k10 t21 n20 k20 n21 r10 xk6
-xk5 xv6 k11 t30 k30 n30 a20 xv5 xv7 xk7 k41 p10 a11 c01 r30 r20 a21 k40 r11 a40 x_x4 r41 p30 k31 c00 a31 p20 c20 r40 r21 r31
-r_x4 p41 k50 c30 c41 p11 c11 k51 k70 c10 k60 p21 a50 r70 r50 p31 p40 a51 k71 r51 a60 c40 p70 a71 p50 p51 r60 c70 k61 r71 c21
-c50 p60 a61 r61 c60 p71 p610 y0 c31 st0 c51 p611 c71 y10 st1 y11 st2"""
+ORDER = """m_w0 l_ex g_pi l_par c_i16 l_up g_c i0 m_bm l_k g_l c_od g_d8 c_i128 c_ci1 g_d i1 c_tw c_al c_u en x_ex r_ex c_H d1 c_h8 c_lo d0
+c_o l_v c_b0 c_be l_q c_b2 c_w0x tw0 l_b tw1 un c_id s0v nw0 f3 f0 f2 f1 s0a xk0 w10 nw1 sx c_ih t01 x_x0 r_x0 w11 n01 s1v xk1
+s1a xv0 xv1 t11 c_b1 c_nh n11 c_bh s2v t10 n10 x_x1 r_x1 s2a xv3 xk3 xv2 k01 t21 t20 k00 xk2 n21 k10 r00 r10 n20 s3v x_x2 r_x2
+p00 p10 x_x3 r_x3 k11 s3a xv5 xk4 xv4 xk5 a01 a11 x_x4 r_x4 r01 r11 t31 t30 n31 k20 n30 k21 k31 xk6 xv7 xk7 xv6 c10 a21 r21 k51
+k50 x_x5 r_x5 p01 p11 r20 k40 k30 p21 r40 p20 c01 c00 a31 a51 a50 k41 r31 r51 a41 c21 c11 p40 c40 c20 k71 a71 k60 r50 k70 r41
+p31 r30 p51 a60 c51 p30 p50 p41 k61 r60 p60 a70 c31 r70 p70 a61 c50 c30 c60 c70 r61 p61 r71 p710 p711 c41 c61 c710 y0 st0 y2 st2
+y1 st1"""
+SEMAPHORES = (["cv", "ca", "cp", "cg", "sent", "r_ex"] + ["r_x%d" % i for i in range(8)] + DMAS
+              + ["z%d%s" % (d, h) for d in range(ND) for h in "01w"])
 
 
-def plan(T, rank, n, peers, cost):
+def plan(T, rank, n, peers):
     ops = []
     serve, asks = rank < n - 1, rank > 0
-    cy, gt = cost["cyc"], cost["gat"]
 
-    def op(name, eng, deps, dur, fn, on=True, lat=0.0, kind="c", nb=0.0):
-        ops.append({"name": name, "eng": eng, "deps": [d for d in deps if d], "dur": dur, "fn": fn, "on": on,
-                    "lat": lat, "kind": kind, "nb": nb / cost["bw"]})
+    def op(name, eng, deps, fn, on=True, kind="c"):
+        ops.append({"name": name, "eng": eng, "deps": [d for d in deps if d], "fn": fn, "on": on, "kind": kind})
         return name
 
-    def vt(w, c=1.0):
-        return max(64, w * c) * cy + 0.03
+    def dma(name, eng, deps, out, in_, on=True):
+        return op(name, eng, deps, lambda e: e.dma_start(out, in_), on, "dma")
 
-    def gat(w):
-        return 0.06 + w * gt * cy
-
-    def dma(name, eng, deps, out, in_, nb, on=True):
-        return op(name, eng, deps, 0.1, lambda e: e.dma_start(out(), in_()), on, cost["dma"], "dma", nb)
-
-    def ts(name, deps, w, out, in0, s1, s2, o0, o1=None, c=1.0):
+    def ts(name, deps, out, in0, s1, s2, o0, o1=None, on=True):
         if o1 is None:
-            return op(name, "v", deps, vt(w, c), lambda e: e.tensor_scalar(out(), in0(), s1(), None, o0))
-        return op(name, "v", deps, vt(w, c), lambda e: e.tensor_scalar(out(), in0(), s1(), s2(), o0, o1))
+            return op(name, "v", deps, lambda e: e.tensor_scalar(out, in0, s1, None, o0), on)
+        return op(name, "v", deps, lambda e: e.tensor_scalar(out, in0, s1, s2, o0, o1), on)
 
-    def aff(name, deps, w, out, in_, scale, bias):
-        return op(name, "a", deps, 0.065 + max(64, w) * cy,
-                  lambda e: e.activation(out(), in_(), F.Identity, bias=bias(), scale=scale()))
+    def tt(name, deps, out, in0, in1, o):
+        return op(name, "v", deps, lambda e: e.tensor_tensor(out, in0, in1, o))
 
-    def k_(x):
-        return lambda: x
+    def aff(name, deps, out, in_, scale=1.0, bias=0.0, func=F.Identity, on=True):
+        return op(name, "a", deps, lambda e: e.activation(out, in_, func, bias=bias, scale=scale), on)
 
-    def v_(name, a, b, step=1):
-        return lambda: T[name][:, a:b:step]
+    def copy(name, deps, out, in_, on=True):
+        return op(name, "v", deps, lambda e: e.tensor_copy(out, in_), on)
+
+    def gather(name, eng, deps, out, win, off, on=True):
+        return (copy if eng == "v" else aff)(name, deps, out, win.indirect(off), on=on)
 
     def col(j):
-        return v_("cf", j, j + 1)
+        return T.cf[:, j:j + 1]
 
-    def copy(name, deps, w, out, in_, on=True):
-        return op(name, "v", deps, vt(w), lambda e: e.tensor_copy(out(), in_()), on)
+    xo = 4 if serve else 0
+    lw = 64 + xo
 
-    def gather(name, eng, deps, w, out, win, off, on=True):
-        if eng == "v":
-            return op(name, "v", deps, gat(w), lambda e: e.tensor_copy(out(), win().indirect(off())), on)
-        return op(name, "a", deps, gat(w), lambda e: e.activation(out(), win().indirect(off()), F.Identity), on)
+    def names(d, a, b):
+        return T.l0[:, a:b] if d == 0 else T.ln[:, lw * (d - 1) + xo + a:lw * (d - 1) + xo + b]
 
-    lw = 68 if serve else 64
-    dma("l_ex", "s", [], v_("ui", 64, 68), lambda: T.ex[:], 20e3, asks)
-    dma("l_par", "a", [], v_("pc", 0, 128), lambda: T.par[:], 64e3)
-    dma("l_up", "s", [], v_("ui", 0, 64), lambda: T.up[:], 32e3)
-    dma("l_k", "a", [], v_("kw", 0, NT), lambda: T.k[:], 512e3)
-    dma("l_b", "s", [], v_("bs", 0, 8), lambda: T.b[:], 20e3)
-    dma("l_v0", "s", [], v_("vw", 0, NT), lambda: T.v[:], 512e3)
-    copy("en", ["l_ex"], 4, v_("xs", 0, 4), v_("ui", 64, 68), asks)
-    for x, dep, land, a, more in (("ex", "en", "ln", 0, cost["first"]), ("es", "es", "ls", 8, 0.0)):
-        op("x_" + x, "g", [dep, "g_d"], 1.0,
-           lambda e, x=x, land=land, a=a: e.remote_dma(T[land][:, 64:68], T.xs[:, a:a + 4], T.sem["r_" + x], T.sem.sent,
-                                                       peers["prev"][1], peers["prev"][0], peers["all"]),
-           asks, cost["rem"] + more - 1.4, kind="rem", nb=100e3)
-        op("r_" + x, "x", ["x_" + x], 0, None, serve, kind="arr")
+    dma("l_par", "s", [], T.pc[:], T.par[:])
+    dma("l_ex", "a", [], T.ui[:, 64:68], T.ex[:], asks)
+    dma("l_up", "a", [], T.ui[:, 0:64], T.up[:])
+    dma("l_k", "a", [], T.kw[:, 0:NT], T.k[:])
+    dma("l_v", "s", ["c_lo"], T.vw[:, 0:NT], T.v[:])
+    dma("l_q", "s", ["c_lo"], T.qs[:], T.q[:])
+    dma("l_b", "s", ["c_lo"], T.bs[:], T.b[:])
+    copy("en", ["l_ex"], T.xs[:, 0:4], T.ui[:, 64:68], asks)
+    op("x_ex", "g", ["en"], lambda e: e.remote_dma(T.xe[:, 0:4], T.xs[:, 0:4], T.sem.r_ex, T.sem.sent,
+                                                   peers["prev"][1], peers["prev"][0], peers["all"]), asks, kind="rem")
+    op("r_ex", "x", ["x_ex"], None, serve, kind="arr")
     fl = {"allow_small_or_imprecise_dtypes": True}
-    op("g_pi", "g", [], 0.15, lambda e: e.iota(T.pi[:, 0:1], [[0, 1]], 0, 1))
-    op("g_l", "g", [], 0.4, lambda e: e.iota(T.l128[:], [[1, 128]], 0, 0, **fl))
-    op("g_d8", "g", [], 0.15, lambda e: e.iota(T.d8[:], [[-16, 8]], 0, 1))
-    op("g_d", "g", [], 0.4, lambda e: e.iota(T.d128[:], [[1, 128]], 0, -1, **fl))
-    op("m_w0", "v", [], vt(NT, 0.5), lambda e: e.memset(T.wt[:, W0:W0 + NT], 0.0))
-    op("m_w1", "v", [], vt(W0 - NT, 0.5), lambda e: e.memset(T.wt[:, NT:W0], 0.0))
-    op("m_bm", "v", [], vt(432, 0.5), lambda e: e.memset(T.bm[:], 0.0))
-    i16, l128 = v_("pi", 1, 2), v_("l128", 0, 128)
-    ts("c_i16", ["g_pi"], 1, i16, v_("pi", 0, 1), k_(15), None, A.bitwise_and)
-    ts("c_i128", ["c_i16"], 1, col(0), i16, k_(128.0), None, A.mult)
-    aff("c_ci0", ["g_l"], 128, v_("ci", 0, 128), l128, k_(1.0), k_(0.0))
-    aff("c_ci1", ["g_l", "c_i128"], 128, v_("ci", 128, 256), l128, k_(0.0), col(0))
+    op("g_pi", "g", [], lambda e: e.iota(T.pi[:, 0:1], [[0, 1]], 0, 1))
+    op("g_c", "g", [], lambda e: e.iota(T.ci[:, 0:128], [[1, 128]], 0, 0, **fl))
+    op("g_l", "g", [], lambda e: e.iota(T.l8[:], [[1, 8]], 0, 0, **fl))
+    op("g_d8", "g", [], lambda e: e.iota(T.d8[:], [[-16, 8]], 0, 1))
+    op("g_d", "g", [], lambda e: e.iota(T.d128[:], [[1, 128]], 0, -1, **fl))
+    op("m_w0", "v", [], lambda e: e.memset(T.wt[:, W0:W0 + NT], 0.0))
+    op("m_bm", "v", [], lambda e: e.memset(T.bm[:], 0.0))
+    c128 = T.ci[:, 0:128]
+    ts("c_i16", ["g_pi"], T.pi[:, 1:2], T.pi[:, 0:1], 15, None, A.bitwise_and)
+    ts("c_i128", ["c_i16"], col(0), T.pi[:, 1:2], 128.0, None, A.mult)
+    aff("c_ci1", ["g_c", "c_i128"], T.ci[:, 128:256], c128, 0.0, col(0))
 
     def row(t):
-        return lambda: T.wt[t:128:16, W0:W0 + NT]
-    dma("i0", "s", ["m_w0", "c_ci0"], row(0), v_("ci", 0, 128), 60e3)
-    dma("i1", "s", ["m_w0", "c_ci1"], row(1), v_("ci", 128, 256), 60e3)
-    ts("c_t1", ["c_i16"], 1, col(4), i16, k_(1.0), k_(1728.0), A.is_equal, A.mult)
-    ts("c_t3", ["c_i16"], 1, col(5), i16, k_(3.0), k_(HB + 1792.0), A.is_equal, A.mult)
-    ts("c_b0", ["c_t1", "c_t3"], 1, col(6), col(4), col(5), k_(128.0), A.add, A.add)
-    ts("c_al", ["c_b0"], 1, col(2), col(6), k_(128.0), None, A.is_equal)
-    ts("c_o", ["c_b0"], 1, col(1), col(6), k_(128.0), k_(128.0), A.is_gt, A.mult)
-    ts("c_w", ["c_al"], 1, col(3), col(2), k_(16.0 - 1.0 / 128), k_(1.0 / 128), A.mult, A.add)
-    aff("c_be", ["c_o", "c_b0", "g_l"], 5, v_("be", 0, 5), v_("l128", 0, 5), col(1), col(6))
-    aff("c_w0x", ["c_be", "c_al"], 64, v_("wt", W0 + NT, W0E), v_("l128", 64, 128), col(2), v_("be", 0, 1))
-    fixed = [aff("f%d" % s, ["m_w1", "c_be", "c_al"], 128, v_("wt", NT + 15 + s, NT + s + 2048, 16), l128, col(2),
-                 v_("be", s + 1, s + 2)) for s in range(4)]
-    h8, d128 = v_("h8", 0, 8), v_("d128", 0, 128)
-    ts("c_h8", ["g_d8"], 8, h8, v_("d8", 0, 8), k_(1), None, A.arith_shift_right)
-    ts("c_b1", ["c_h8", "m_bm"], 8, v_("bm", 15, 143, 16), h8, k_(0.0), None, A.is_equal)
-    ts("c_b2", ["c_h8", "m_bm"], 8, v_("bm", 159, 287, 16), h8, k_(1.0), None, A.is_equal)
-    ts("c_b3", ["c_h8", "m_bm", "c_w"], 8, v_("bm", 303, 431, 16), h8, k_(1.0), col(3), A.is_equal, A.mult)
-    ts("c_id", ["g_d"], 128, v_("idb", 0, 128), d128, k_(0.0), None, A.is_equal)
-    ts("c_ih", ["g_d"], 128, v_("idh", 0, 128), d128, k_(0.0), None, A.is_equal)
-    ts("c_nh", ["g_d"], 128, v_("idh", 128, 256), d128, k_(0.0), k_(-1.0), A.is_equal, A.mult)
-    copy("c_bh", ["l_b"], 8, v_("bh", 0, 8), v_("bs", 0, 8))
-    pc, lo_, hi_ = v_("pc", 0, 128), v_("dg", 0, 128), v_("dg", 128, 256)
-    ts("c_H", ["l_par"], 128, hi_, pc, k_(2047.0), k_(HB - 63.5), A.min, A.add)
-    ts("c_pf", ["l_par"], 128, v_("pf", 0, 128), pc, k_(HB), None, A.add)
-    op("c_lo", "v", ["c_H", "c_pf"], vt(256), lambda e: e.tensor_tensor(lo_(), T.pf[:], hi_(), A.subtract))
-    dma("d1", "a", ["m_w0", "c_H"], row(3), hi_, 60e3)
-    dma("d0", "s", ["m_w0", "c_lo"], row(2), lo_, 60e3)
-    dma("l_q", "s", ["d0"], v_("qs", 0, NC), lambda: T.q[:], 256e3)
-    copy("c_pl", ["l_par"], 128, v_("pl", 0, 128), pc)
-    copy("un", ["l_up"], 64, v_("ln", 0, 64), v_("ui", 0, 64))
-    uw = 68 if asks else 64
-    ts("uh", ["l_up", "l_ex"], 68, v_("uh", 0, uw), v_("ui", 0, uw), k_(7), None, A.arith_shift_right)
-    ts("uu", ["uh"], 68, v_("uu", 0, uw), v_("uh", 0, uw), k_(15.0), k_(-2047.0 / 16), A.min, A.mult)
-    op("uw", "v", ["uu"], vt(136), lambda e: e.tensor_tensor(T.uw[:, 0:uw], T.uu[:, 0:uw], T.ui[:, 0:uw], A.add))
-    op("es", "v", ["uw"], vt(4), lambda e: e.tensor_scalar(T.xs[:, 8:12], T.uw[:, 64:68], 16.0, None, A.mult), asks)
-    ts("us", ["uw"], 64, v_("ls", 0, 64), v_("uw", 0, 64), k_(16.0), None, A.mult)
-    w0 = ["i0", "i1", "d0", "d1", "c_w0x", "c_pl"]
-    w1 = fixed + [gather("w1%d" % i, q, w0, 16 * (b - a), v_("wt", 16 * a, 16 * b), v_("wt", W0, W0E), v_("pl", a, b))
-                  for i, (q, a, b) in enumerate(CFG["w1"])]
-    lists = {0: "un"}
-    last_s, bank_free = ["us", "r_es"], [None, None, None]
-    for j in range(4):
-        c, win, x, y = CFG["s"][j], v_("wt", 0, W0), 1088 * j, 72 * j
-        got = []
-        if c:
-            got.append(gather("s%dv" % j, "v", w1 + last_s, 16 * min(c, 68), v_("res", x, x + 16 * min(c, lw)), win,
-                              v_("ls", y, y + min(c, lw))))
-        if c < 64:
-            got.append(gather("s%da" % j, "a", w1 + last_s, 16 * (68 - c), v_("res", x + 16 * c, x + 16 * lw), win,
-                              v_("ls", y + c, y + lw)))
-        for kind in ([2, 0, 1] if j < 3 else [0]):
-            ps = v_("pl%d" % kind, 0, lw)
+        return T.wt[t:128:16, W0:W0 + NT]
+    dma("i0", "s", ["m_w0", "g_c"], row(0), c128)
+    dma("i1", "s", ["m_w0", "c_ci1"], row(1), T.ci[:, 128:256])
+    ts("c_od", ["g_pi"], T.pi[:, 2:3], T.pi[:, 0:1], 1, None, A.bitwise_and)
+    ts("c_tw", ["g_pi"], T.pi[:, 3:4], T.pi[:, 0:1], 2, None, A.bitwise_and)
+    ts("c_al", ["c_od"], col(2), T.pi[:, 2:3], -1.0, 1.0, A.mult, A.add)
+    ts("c_o", ["c_od"], col(1), T.pi[:, 2:3], 128.0, None, A.mult)
+    ts("c_u", ["c_tw"], col(4), T.pi[:, 3:4], 32.0, 64.0 - 1920.0, A.mult, A.add)
+    ts("c_b0", ["c_u", "c_al"], col(5), col(4), col(2), 1920.0, A.mult, A.add)
+    aff("c_be", ["c_o", "c_b0", "g_l"], T.be[:, 0:5], T.l8[:, 0:5], col(1), col(5))
+    aff("c_w0x", ["c_be", "g_c"], T.wt[:, W0 + NT:W0E], T.ci[:, 64:128], col(2), T.be[:, 0:1])
+    fixed = [aff("f%d" % s, ["c_be", "g_c"], T.wt[:, NT + 128 * s:NT + 128 * s + 128], c128, col(2), T.be[:, s + 1:s + 2])
+             for s in range(4)]
+    ts("c_h8", ["g_d8"], T.h8[:], T.d8[:], 1, None, A.arith_shift_right)
+    ts("c_b1", ["c_h8", "m_bm"], T.bm[:, 15:143:16], T.h8[:], 0.0, None, A.is_equal)
+    ts("c_b2", ["c_h8", "m_bm"], T.bm[:, 159:287:16], T.h8[:], 1.0, None, A.is_equal)
+    ts("c_id", ["g_d"], T.idb[:], T.d128[:], 0.0, None, A.is_equal)
+    ts("c_ih", ["g_d"], T.idh[:, 0:128], T.d128[:], 0.0, None, A.is_equal)
+    ts("c_nh", ["g_d"], T.idh[:, 128:256], T.d128[:], 0.0, -1.0, A.is_equal, A.mult)
+    copy("c_bh", ["l_b"], T.bh[:], T.bs[:])
+    lo_, hi_ = T.dg[:, 0:128], T.dg[:, 128:256]
+    copy("c_H", ["l_par"], hi_, T.pc[:])
+    tt("c_lo", ["c_H"], lo_, T.pc[:], hi_, A.subtract)
+    dma("d1", "a", ["m_w0", "c_H"], row(3), hi_)
+    dma("d0", "s", ["m_w0", "c_lo"], row(2), lo_)
+    copy("un", ["l_up"], names(0, 0, 64), T.ui[:, 0:64])
 
-            def relay(e, x=x, kind=kind, ps=ps):
-                for i in range(16):
-                    r = e.matmul(ps(), T.bm[:, 144 * kind + 15 - i:144 * kind + 143 - i], T.res[:, x + i:x + 16 * lw:16],
-                                 i == 0, i == 15)
-                return r
-            m = op("t%d%d" % (j, kind), "p", got + ["c_b%d" % (kind + 1), bank_free[kind]], 16 * (68 * cost["pe"] + 0.005), relay)
-            d = 2 * j + 1 + kind
-            out = v_("ls", y + 72, y + 72 + lw) if kind == 2 else v_("ln", 72 * d, 72 * d + lw)
-            bank_free[kind] = ts("n%d%d" % (j, kind), [m], 68, out, ps, k_([0.0, -HB, -HB / 128][kind]), None, A.add)
-            if kind == 2:
-                last_s = [bank_free[kind]]
-            else:
-                lists[d] = bank_free[kind]
+    def relay(name, deps, kind, ps, src, x, w, out, on=True):
+        def calls(e):
+            for i in range(16):
+                r = e.matmul(ps[:, 0:w], T.bm[:, 144 * kind + 15 - i:144 * kind + 143 - i], src[:, x + i:x + 16 * w:16], i == 0, i == 15)
+            return r
+        return copy("n" + name, [op("t" + name, "p", deps + ["c_b%d" % (kind + 1)], calls, on)], out, ps[:, 0:w], on)
+    w0 = ["i0", "i1", "d0", "d1"]
+    free = [relay("w%d" % i, w0, 1, [T.pla, T.plb][i], T.wt, W0 + 16 * a, b - a, T.pl[:, a:b]) for i, (q, a, b) in enumerate(CFG["w1"])]
+    w1 = [gather("w1%d" % i, q, [free[i], "c_w0x"], T.wt[:, 16 * a:16 * b], T.wt[:, W0:W0E], T.pl[:, a:b])
+          for i, (q, a, b) in enumerate(CFG["w1"])]
+    lists = {0: "un"}
+    for j in range(4):
+        c, x, d, o = min(CFG["s"][j], lw), 1088 * j, max(2 * j - 1, 0), (0 if j else xo)
+        deps, win = ([lists[d]] + w1 + fixed, T.wt[:, 0:W0]) if j else (w0 + ["un", "c_w0x"], T.wt[:, W0:W0E])
+        got = []
+        if not j:
+            got.append(gather("sx", "v" if "x" in CFG["xv"] else "a", w0 + ["r_ex"], T.res[:, 0:64], T.wt[:, W0:W0 + NT], T.xe[:, 0:4], serve))
+        if c > o:
+            got.append(gather("s%dv" % j, "v", deps, T.res[:, x + 16 * o:x + 16 * c], win, names(d, o - xo, c - xo)))
+        if c < 64:
+            got.append(gather("s%da" % j, "a", deps, T.res[:, x + 16 * max(c, o):x + 16 * lw], win, names(d, max(c, o) - xo, 64)))
+        for kind in ([1, 0] if j else [1]):
+            free[kind] = lists[2 * j + kind] = relay("%d%d" % (j, kind), got + [free[kind]], kind, [T.pla, T.plb][kind], T.res, x, lw,
+                                                     names(2 * j + kind, -xo, 64))
     have = {}
-    loads = {"k": ["l_k"], "v": ["l_v0"]}
-    for i, (which, a, b) in enumerate(SENDS):
+    for i, (which, a, b) in enumerate(CFG["sends"]):
         got = []
         for d in range(a, b):
+            ready, off = ("r_ex", T.xe[:, 0:4]) if d == 0 else (lists[d], names(d, -4, 0))
             for x in which:
-                got.append(gather("x%s%d" % (x, d), "v" if "%s%d" % (x, d) in CFG["xv"] else "a",
-                                  ["r_ex" if d == 0 else lists[d]] + loads[x], 64, v_("x" + x, 64 * d, 64 * d + 64),
-                                  v_(x + "w", 0, NT), v_("ln", 72 * d + 64, 72 * d + 68), serve))
+                got.append(gather("x%s%d" % (x, d), "v" if "%s%d" % (x, d) in CFG["xv"] else "a", [ready, "l_" + x],
+                                  T["x" + x][:, 64 * d:64 * d + 64], T[x + "w"][:, 0:NT], off, serve))
                 have[x, d] = have.get((x, d - 1), []) + ["r_x%d" % i]
 
         def give(e, i=i, which=which, a=a, b=b):
@@ -194,65 +164,73 @@ def plan(T, rank, n, peers, cost):
                 [RemoteDMATransfer(dst_ids=[dst], dma_engine_mask=masks[u], remote_sem=T.sem["r_x%d" % i],
                                    src=T["x" + x][:, 64 * a:64 * b], dst=T[x + "w"][:, NT + 64 * a:NT + 64 * b])
                  for u, x in enumerate(which)], local_sem=T.sem.sent)
-        op("x_x%d" % i, "g", got, 1.0, give, serve, cost["rem"] - 1.4 + (cost["first"] * 0.5 if i == 0 else 0.0),
-           kind="rem", nb=120e3 * len(which))
-        op("r_x%d" % i, "x", ["x_x%d" % i], 0, None, asks, kind="arr")
+        op("x_x%d" % i, "g", got, give, serve, kind="rem")
+        op("r_x%d" % i, "x", ["x_x%d" % i], None, asks, kind="arr")
     items = CFG["items"].split()
-    acc, xfree, nx, added = [[], []], [None, None, None], 0, [0, 0]
+    acc, xfree, nx, added = [[], [], []], [None] * 4, 0, [0, 0, 0]
+
+    def adds(name, deps, d, a, w, neg):
+        part = [u for u, (_, x, z) in enumerate(ACC) if a <= x < a + w]
+
+        def calls(e):
+            for u in part:
+                bank, x, z = ACC[u]
+                added[u] += 1
+                r = e.matmul(T[bank][:, 0:z], T.idh[:, 128 * neg:128 * neg + 128], T.pb[:, NC * d + x:NC * d + x + z],
+                             added[u] == 1, added[u] == ND - (u == 2))
+            return r
+        op(name, "p", deps + ["c_nh" if neg else "c_ih"] + ([free[1]] if 2 in part else []), calls)
+        for u in part:
+            acc[u].append(name)
+
     for z, (d, h, way) in enumerate(items):
         t, d = d + h, int(d)
         a, w = (0, NC) if h == "w" else (512 * int(h), 512)
         lo, ww = NC * d + a, (NT + NE * (d + 1) if asks else NT)
 
         def pick(x, a, w, d=d, ww=ww):
-            return T[x][:, 0:ww].indirect(T.ln[:, 72 * d + a // 16:72 * d + (a + w) // 16])
-        xb, rb, qs = v_("xb", lo, lo + w), v_("rb", lo, lo + w), v_("qs", a, a + w)
+            return T[x][:, 0:ww].indirect(names(d, a // 16, (a + w) // 16))
+        xb, rb, qs = T.xb[:, lo:lo + w], T.rb[:, lo:lo + w], T.qs[:, a:a + w]
         src = [lists[d], "l_k"] + have["k", d]
         if way == "v":
-            op("k" + t, "v", src + ["l_q"], gat(w),
-               lambda e, xb=xb, qs=qs, pick=pick, a=a, w=w: e.tensor_tensor(xb(), pick("kw", a, w), qs(), A.subtract))
-            clamped = [ts("r" + t, ["k" + t, "c_bh"], w, rb, xb, v_("bh", d, d + 1), k_(0.0), A.subtract, A.min, c=0.5)]
+            tt("k" + t, src + ["l_q"], xb, pick("kw", a, w), qs, A.subtract)
+            clamped = [ts("r" + t, ["k" + t, "c_bh"], rb, xb, T.bh[:, d:d + 1], 0.0, A.subtract, A.min)]
         else:
-            op("k" + t, "a", src + ["l_b"], gat(w),
-               lambda e, xb=xb, pick=pick, a=a, w=w, d=d: e.activation(xb(), pick("kw", a, w), F.Identity,
-                                                                       bias=T.bs[:, d:d + 1], scale=-1.0))
-            clamped = []
-            for u in range(a // 512, (a + w) // 512):
-                px, x, tu = v_("px%d" % nx, 0, 512), NC * d + 512 * u, "%d%d" % (d, u)
+            aff("k" + t, src + ["l_b"], xb, pick("kw", a, w), -1.0, T.bs[:, d:d + 1])
+        if way == "z":
+            op("z" + t, "g", ["k" + t, "l_q"], lambda e, xb=xb, qs=qs: e.dma_start(xb, qs, accum_op=A.add), kind="dma")
+            clamped = [ts("r" + t, ["z" + t], rb, xb, 0.0, None, A.max)]
+        if way == "p":
+            nx = (nx + (nx % 2 if w == NC else 0)) % 4
+            banks, px = range(nx, nx + w // 512), T["px%d" % (nx // 2)][:, 512 * (nx % 2):512 * (nx % 2) + w]
 
-                def addq(e, px=px, x=x, u=u):
-                    e.matmul(px(), T.idb[:], T.qs[:, 512 * u:512 * u + 512], True, False)
-                    return e.matmul(px(), T.idb[:], T.xb[:, x:x + 512], False, True)
-                op("a" + tu, "p", ["k" + t, "l_q", "c_id", xfree[nx]], 1024 * cost["pe"] + 0.05, addq)
-                xfree[nx] = op("r" + tu, "a", ["a" + tu], 0.065 + 512 * cy,
-                               lambda e, px=px, x=x: e.activation(T.rb[:, x:x + 512], px(), F.Relu))
-                clamped.append(xfree[nx])
-                nx = (nx + 1) % 3
-        vsrc = [lists[d]] + clamped + loads["v"] + have["v", d]
+            def addq(e, nx=nx, lo=lo, a=a, w=w):
+                for x in range(0, w, 512):
+                    to = T["px%d" % (nx // 2)][:, 512 * (nx % 2) + x:512 * (nx % 2) + x + 512]
+                    e.matmul(to, T.idb[:], T.qs[:, a + x:a + x + 512], True, False)
+                    r = e.matmul(to, T.idb[:], T.xb[:, lo + x:lo + x + 512], False, True)
+                return r
+            op("a" + t, "p", ["k" + t, "l_q", "c_id"] + [xfree[u] for u in banks], addq)
+            clamped = [aff("r" + t, ["a" + t], rb, px, func=F.Relu)]
+            for u in banks:
+                xfree[u] = clamped[0]
+            nx = (nx + w // 512) % 4
+        vsrc = [lists[d], "l_v"] + clamped + have["v", d]
         neg = int(way == "v")
 
         def times(name, a, w, d=d, pick=pick, vsrc=vsrc):
             x = NC * d + a
-            return op(name, "v", vsrc, gat(w),
-                      lambda e: e.tensor_tensor(T.pb[:, x:x + w], pick("vw", a, w), T.rb[:, x:x + w], A.mult))
+            return tt(name, vsrc, T.pb[:, x:x + w], pick("vw", a, w), T.rb[:, x:x + w], A.mult)
         if z < len(items) - 1:
-            times("p" + t, a, w)
-            for u in range(a // 512, (a + w) // 512):
-                def add(e, u=u, x=NC * d + 512 * u, neg=neg):
-                    added[u] += 1
-                    return e.matmul(T["acc%d" % u][:], T.idh[:, 128 * neg:128 * neg + 128], T.pb[:, x:x + 512],
-                                    added[u] == 1, added[u] == ND - u)
-                acc[u].append(op("c%d%d" % (d, u), "p", ["p" + t, "c_nh" if neg else "c_ih"], 512 * cost["pe"] + 0.03, add))
+            adds("c" + t, [times("p" + t, a, w)], d, a, w, neg)
         else:
-            aff("y0", acc[0], 512, v_("ys", 0, 512), v_("acc0", 0, 512), k_(1.0), k_(0.0))
-            dma("st0", "s", ["y0"], v_("y", 0, 512), v_("ys", 0, 512), 256e3)
-            for u in range(2):
-                x = 512 + 256 * u
-                op("y1%d" % u, "v", [times("p%s%d" % (t, u), x, 256)] + acc[1], vt(256),
-                   lambda e, x=x, d=d, neg=neg: e.tensor_tensor(
-                       T.ys[:, x:x + 256], T.acc1[:, x - 512:x - 256], T.pb[:, NC * d + x:NC * d + x + 256],
-                       A.subtract if neg else A.add))
-                dma("st%d" % (u + 1), "sa"[u], ["y1%d" % u], v_("y", x, x + 256), v_("ys", x, x + 256), 128e3)
+            adds("c%s0" % t, [times("p%s0" % t, 512, 256)], d, 512, 256, neg)
+            tt("y2", [times("p%s1" % t, 768, 256)] + acc[2], T.ys[:, 768:NC], T.plb[:, 0:256], T.pb[:, NC * d + 768:NC * d + NC],
+               A.subtract if neg else A.add)
+    for u, (bank, x, z) in enumerate(ACC):
+        if u < 2:
+            aff("y%d" % u, acc[u], T.ys[:, x:x + z], T[bank][:, 0:z])
+        dma("st%d" % u, "sas"[u], ["y%d" % u], T.y[:, x:x + z], T.ys[:, x:x + z])
     return ops
 
 
@@ -269,12 +247,14 @@ def rank_program(g, core, T, topo):
         peers["prev"] = topo.addr(T.cores[rank - 1], core)
     if rank < n - 1:
         peers["next"] = topo.addr(T.cores[rank + 1], core)
-    ops = {o["name"]: o for o in plan(T, rank, n, peers, COST) if o["on"]}
+    ops = {o["name"]: o for o in plan(T, rank, n, peers) if o["on"]}
     needed = {d for o in ops.values() for d in o["deps"]}
     queue = {"v": g.vector, "a": g.scalar, "p": g.tensor, "g": g, "s": g.sync}
     count = {"v": 0, "a": 0, "p": 0, "g": 0}
     mark, seen, sent = {}, {q: {} for q in queue}, 0
-    for name in ORDER.split():
+    order = ORDER.split()
+    assert all(name in order for name in ops)
+    for name in order:
         if name not in ops:
             continue
         o = ops[name]
@@ -284,7 +264,8 @@ def rank_program(g, core, T, topo):
         e = queue[o["eng"]]
         want = {}
         for d in o["deps"]:
-            if d in mark and not (o["eng"] in "pg" and ops[d]["eng"] == o["eng"]):
+            assert d in mark or d not in ops
+            if d in mark and not (o["eng"] == "p" == ops[d]["eng"]):
                 s, v = mark[d]
                 want[s] = max(want.get(s, 0), v)
         for s, v in want.items():

from concourse.bass import DstId, RemoteDMATransfer
from concourse.mybir import AluOpType as A, ActivationFunctionType as F

NT, NC, NE, ND = 2048, 1024, 64, 8
KW = NT + NE * ND
W0, W0E = KW, KW + NT + NE
BF, F32, I32, U16 = "bfloat16", "float32", "int32", "uint16"
SCRATCH = {n: ("sbuf", [128, w], t) for n, w, t in [
    ("kw", KW, BF), ("vw", KW, BF), ("qs", NC, BF), ("bs", 8, F32), ("bh", 8, BF), ("wt", W0E, BF),
    ("pc", 128, I32), ("pl", 128, U16), ("dg", 256, BF), ("ci", 256, BF),
    ("ui", 72, I32), ("xs", 8, U16), ("xe", 8, U16), ("l0", 64, U16), ("ln", 7 * 68, U16),
    ("res", 4 * 1088, BF), ("xk", 512, BF), ("xv", 512, BF),
    ("pi", 8, I32), ("d8", 8, I32), ("h8", 8, I32), ("l8", 8, F32), ("d128", 128, F32), ("cf", 8, F32), ("be", 8, F32),
    ("bm", 2 * 144, BF), ("idb", 128, BF), ("idh", 256, "float16"),
    ("xb", ND * NC, BF), ("rb", ND * NC, BF), ("pb", ND * NC, "float16"), ("ys", NC, F32)]}
SCRATCH.update({n: ("psum", [128, w], F32) for n, w in [("px0", NC), ("px1", NC), ("acc0", 512), ("acc1", 512), ("pla", 512), ("plb", 512)]})
ACC = [("acc0", 0, 512), ("acc1", 512, 256), ("plb", 768, 256)]
DMAS = ["l_ex", "l_up", "l_par", "l_b", "l_k", "l_v", "l_q", "i0", "i1", "d0", "d1", "st0", "st1", "st2"]
CFG = {
    "sends": [("k", 0, 1), ("k", 1, 2), ("v", 0, 2), ("kv", 2, 4), ("kv", 4, 6), ("kv", 6, 8)],
    "w1": [("a", 0, 70), ("v", 70, 128)],
    "s": [36, 34, 34, 14],
    "xv": ["x", "k1", "k2"],
    "items": "00v 01p 10v 11p 20v 21p 30v 31p 40v 41p 50p 51p 60p 61p 70p 71p",
}
ORDER = """m_w0 l_ex g_pi l_par c_i16 l_up g_c i0 m_bm l_k g_l c_od g_d8 c_i128 c_ci1 g_d i1 c_tw c_al c_u en x_ex r_ex c_H d1 c_h8 c_lo d0
c_o l_v c_b0 c_be l_q c_b2 c_w0x tw0 l_b tw1 un c_id s0v nw0 f3 f0 f2 f1 s0a xk0 w10 nw1 sx c_ih t01 x_x0 r_x0 w11 n01 s1v xk1
s1a xv0 xv1 t11 c_b1 c_nh n11 c_bh s2v t10 n10 x_x1 r_x1 s2a xv3 xk3 xv2 k01 t21 t20 k00 xk2 n21 k10 r00 r10 n20 s3v x_x2 r_x2
p00 p10 x_x3 r_x3 k11 s3a xv5 xk4 xv4 xk5 a01 a11 x_x4 r_x4 r01 r11 t31 t30 n31 k20 n30 k21 k31 xk6 xv7 xk7 xv6 c10 a21 r21 k51
k50 x_x5 r_x5 p01 p11 r20 k40 k30 p21 r40 p20 c01 c00 a31 a51 a50 k41 r31 r51 a41 c21 c11 p40 c40 c20 k71 a71 k60 r50 k70 r41
p31 r30 p51 a60 c51 p30 p50 p41 k61 r60 p60 a70 c31 r70 p70 a61 c50 c30 c60 c70 r61 p61 r71 p710 p711 c41 c61 c710 y0 st0 y2 st2
y1 st1"""
SEMAPHORES = (["cv", "ca", "cp", "cg", "sent", "r_ex"] + ["r_x%d" % i for i in range(8)] + DMAS
              + ["z%d%s" % (d, h) for d in range(ND) for h in "01w"])


def plan(T, rank, n, peers):
    ops = []
    serve, asks = rank < n - 1, rank > 0

    def op(name, eng, deps, fn, on=True, kind="c"):
        ops.append({"name": name, "eng": eng, "deps": [d for d in deps if d], "fn": fn, "on": on, "kind": kind})
        return name

    def dma(name, eng, deps, out, in_, on=True):
        return op(name, eng, deps, lambda e: e.dma_start(out, in_), on, "dma")

    def ts(name, deps, out, in0, s1, s2, o0, o1=None, on=True):
        if o1 is None:
            return op(name, "v", deps, lambda e: e.tensor_scalar(out, in0, s1, None, o0), on)
        return op(name, "v", deps, lambda e: e.tensor_scalar(out, in0, s1, s2, o0, o1), on)

    def tt(name, deps, out, in0, in1, o):
        return op(name, "v", deps, lambda e: e.tensor_tensor(out, in0, in1, o))

    def aff(name, deps, out, in_, scale=1.0, bias=0.0, func=F.Identity, on=True):
        return op(name, "a", deps, lambda e: e.activation(out, in_, func, bias=bias, scale=scale), on)

    def copy(name, deps, out, in_, on=True):
        return op(name, "v", deps, lambda e: e.tensor_copy(out, in_), on)

    def gather(name, eng, deps, out, win, off, on=True):
        return (copy if eng == "v" else aff)(name, deps, out, win.indirect(off), on=on)

    def col(j):
        return T.cf[:, j:j + 1]

    xo = 4 if serve else 0
    lw = 64 + xo

    def names(d, a, b):
        return T.l0[:, a:b] if d == 0 else T.ln[:, lw * (d - 1) + xo + a:lw * (d - 1) + xo + b]

    dma("l_par", "s", [], T.pc[:], T.par[:])
    dma("l_ex", "a", [], T.ui[:, 64:68], T.ex[:], asks)
    dma("l_up", "a", [], T.ui[:, 0:64], T.up[:])
    dma("l_k", "a", [], T.kw[:, 0:NT], T.k[:])
    dma("l_v", "s", ["c_lo"], T.vw[:, 0:NT], T.v[:])
    dma("l_q", "s", ["c_lo"], T.qs[:], T.q[:])
    dma("l_b", "s", ["c_lo"], T.bs[:], T.b[:])
    copy("en", ["l_ex"], T.xs[:, 0:4], T.ui[:, 64:68], asks)
    op("x_ex", "g", ["en"], lambda e: e.remote_dma(T.xe[:, 0:4], T.xs[:, 0:4], T.sem.r_ex, T.sem.sent,
                                                   peers["prev"][1], peers["prev"][0], peers["all"]), asks, kind="rem")
    op("r_ex", "x", ["x_ex"], None, serve, kind="arr")
    fl = {"allow_small_or_imprecise_dtypes": True}
    op("g_pi", "g", [], lambda e: e.iota(T.pi[:, 0:1], [[0, 1]], 0, 1))
    op("g_c", "g", [], lambda e: e.iota(T.ci[:, 0:128], [[1, 128]], 0, 0, **fl))
    op("g_l", "g", [], lambda e: e.iota(T.l8[:], [[1, 8]], 0, 0, **fl))
    op("g_d8", "g", [], lambda e: e.iota(T.d8[:], [[-16, 8]], 0, 1))
    op("g_d", "g", [], lambda e: e.iota(T.d128[:], [[1, 128]], 0, -1, **fl))
    op("m_w0", "v", [], lambda e: e.memset(T.wt[:, W0:W0 + NT], 0.0))
    op("m_bm", "v", [], lambda e: e.memset(T.bm[:], 0.0))
    c128 = T.ci[:, 0:128]
    ts("c_i16", ["g_pi"], T.pi[:, 1:2], T.pi[:, 0:1], 15, None, A.bitwise_and)
    ts("c_i128", ["c_i16"], col(0), T.pi[:, 1:2], 128.0, None, A.mult)
    aff("c_ci1", ["g_c", "c_i128"], T.ci[:, 128:256], c128, 0.0, col(0))

    def row(t):
        return T.wt[t:128:16, W0:W0 + NT]
    dma("i0", "s", ["m_w0", "g_c"], row(0), c128)
    dma("i1", "s", ["m_w0", "c_ci1"], row(1), T.ci[:, 128:256])
    ts("c_od", ["g_pi"], T.pi[:, 2:3], T.pi[:, 0:1], 1, None, A.bitwise_and)
    ts("c_tw", ["g_pi"], T.pi[:, 3:4], T.pi[:, 0:1], 2, None, A.bitwise_and)
    ts("c_al", ["c_od"], col(2), T.pi[:, 2:3], -1.0, 1.0, A.mult, A.add)
    ts("c_o", ["c_od"], col(1), T.pi[:, 2:3], 128.0, None, A.mult)
    ts("c_u", ["c_tw"], col(4), T.pi[:, 3:4], 32.0, 64.0 - 1920.0, A.mult, A.add)
    ts("c_b0", ["c_u", "c_al"], col(5), col(4), col(2), 1920.0, A.mult, A.add)
    aff("c_be", ["c_o", "c_b0", "g_l"], T.be[:, 0:5], T.l8[:, 0:5], col(1), col(5))
    aff("c_w0x", ["c_be", "g_c"], T.wt[:, W0 + NT:W0E], T.ci[:, 64:128], col(2), T.be[:, 0:1])
    fixed = [aff("f%d" % s, ["c_be", "g_c"], T.wt[:, NT + 128 * s:NT + 128 * s + 128], c128, col(2), T.be[:, s + 1:s + 2])
             for s in range(4)]
    ts("c_h8", ["g_d8"], T.h8[:], T.d8[:], 1, None, A.arith_shift_right)
    ts("c_b1", ["c_h8", "m_bm"], T.bm[:, 15:143:16], T.h8[:], 0.0, None, A.is_equal)
    ts("c_b2", ["c_h8", "m_bm"], T.bm[:, 159:287:16], T.h8[:], 1.0, None, A.is_equal)
    ts("c_id", ["g_d"], T.idb[:], T.d128[:], 0.0, None, A.is_equal)
    ts("c_ih", ["g_d"], T.idh[:, 0:128], T.d128[:], 0.0, None, A.is_equal)
    ts("c_nh", ["g_d"], T.idh[:, 128:256], T.d128[:], 0.0, -1.0, A.is_equal, A.mult)
    copy("c_bh", ["l_b"], T.bh[:], T.bs[:])
    lo_, hi_ = T.dg[:, 0:128], T.dg[:, 128:256]
    copy("c_H", ["l_par"], hi_, T.pc[:])
    tt("c_lo", ["c_H"], lo_, T.pc[:], hi_, A.subtract)
    dma("d1", "a", ["m_w0", "c_H"], row(3), hi_)
    dma("d0", "s", ["m_w0", "c_lo"], row(2), lo_)
    copy("un", ["l_up"], names(0, 0, 64), T.ui[:, 0:64])

    def relay(name, deps, kind, ps, src, x, w, out, on=True):
        def calls(e):
            for i in range(16):
                r = e.matmul(ps[:, 0:w], T.bm[:, 144 * kind + 15 - i:144 * kind + 143 - i], src[:, x + i:x + 16 * w:16], i == 0, i == 15)
            return r
        return copy("n" + name, [op("t" + name, "p", deps + ["c_b%d" % (kind + 1)], calls, on)], out, ps[:, 0:w], on)
    w0 = ["i0", "i1", "d0", "d1"]
    free = [relay("w%d" % i, w0, 1, [T.pla, T.plb][i], T.wt, W0 + 16 * a, b - a, T.pl[:, a:b]) for i, (q, a, b) in enumerate(CFG["w1"])]
    w1 = [gather("w1%d" % i, q, [free[i], "c_w0x"], T.wt[:, 16 * a:16 * b], T.wt[:, W0:W0E], T.pl[:, a:b])
          for i, (q, a, b) in enumerate(CFG["w1"])]
    lists = {0: "un"}
    for j in range(4):
        c, x, d, o = min(CFG["s"][j], lw), 1088 * j, max(2 * j - 1, 0), (0 if j else xo)
        deps, win = ([lists[d]] + w1 + fixed, T.wt[:, 0:W0]) if j else (w0 + ["un", "c_w0x"], T.wt[:, W0:W0E])
        got = []
        if not j:
            got.append(gather("sx", "v" if "x" in CFG["xv"] else "a", w0 + ["r_ex"], T.res[:, 0:64], T.wt[:, W0:W0 + NT], T.xe[:, 0:4], serve))
        if c > o:
            got.append(gather("s%dv" % j, "v", deps, T.res[:, x + 16 * o:x + 16 * c], win, names(d, o - xo, c - xo)))
        if c < 64:
            got.append(gather("s%da" % j, "a", deps, T.res[:, x + 16 * max(c, o):x + 16 * lw], win, names(d, max(c, o) - xo, 64)))
        for kind in ([1, 0] if j else [1]):
            free[kind] = lists[2 * j + kind] = relay("%d%d" % (j, kind), got + [free[kind]], kind, [T.pla, T.plb][kind], T.res, x, lw,
                                                     names(2 * j + kind, -xo, 64))
    have = {}
    for i, (which, a, b) in enumerate(CFG["sends"]):
        got = []
        for d in range(a, b):
            ready, off = ("r_ex", T.xe[:, 0:4]) if d == 0 else (lists[d], names(d, -4, 0))
            for x in which:
                got.append(gather("x%s%d" % (x, d), "v" if "%s%d" % (x, d) in CFG["xv"] else "a", [ready, "l_" + x],
                                  T["x" + x][:, 64 * d:64 * d + 64], T[x + "w"][:, 0:NT], off, serve))
                have[x, d] = have.get((x, d - 1), []) + ["r_x%d" % i]

        def give(e, i=i, which=which, a=a, b=b):
            dst = DstId(rid=peers["next"][0], pnc=peers["next"][1])
            masks = peers["half"] if len(which) == 2 else [peers["all"]]
            return e.remote_dma_fused(
                [RemoteDMATransfer(dst_ids=[dst], dma_engine_mask=masks[u], remote_sem=T.sem["r_x%d" % i],
                                   src=T["x" + x][:, 64 * a:64 * b], dst=T[x + "w"][:, NT + 64 * a:NT + 64 * b])
                 for u, x in enumerate(which)], local_sem=T.sem.sent)
        op("x_x%d" % i, "g", got, give, serve, kind="rem")
        op("r_x%d" % i, "x", ["x_x%d" % i], None, asks, kind="arr")
    items = CFG["items"].split()
    acc, xfree, nx, added = [[], [], []], [None] * 4, 0, [0, 0, 0]

    def adds(name, deps, d, a, w, neg):
        part = [u for u, (_, x, z) in enumerate(ACC) if a <= x < a + w]

        def calls(e):
            for u in part:
                bank, x, z = ACC[u]
                added[u] += 1
                r = e.matmul(T[bank][:, 0:z], T.idh[:, 128 * neg:128 * neg + 128], T.pb[:, NC * d + x:NC * d + x + z],
                             added[u] == 1, added[u] == ND - (u == 2))
            return r
        op(name, "p", deps + ["c_nh" if neg else "c_ih"] + ([free[1]] if 2 in part else []), calls)
        for u in part:
            acc[u].append(name)

    for z, (d, h, way) in enumerate(items):
        t, d = d + h, int(d)
        a, w = (0, NC) if h == "w" else (512 * int(h), 512)
        lo, ww = NC * d + a, (NT + NE * (d + 1) if asks else NT)

        def pick(x, a, w, d=d, ww=ww):
            return T[x][:, 0:ww].indirect(names(d, a // 16, (a + w) // 16))
        xb, rb, qs = T.xb[:, lo:lo + w], T.rb[:, lo:lo + w], T.qs[:, a:a + w]
        src = [lists[d], "l_k"] + have["k", d]
        if way == "v":
            tt("k" + t, src + ["l_q"], xb, pick("kw", a, w), qs, A.subtract)
            clamped = [ts("r" + t, ["k" + t, "c_bh"], rb, xb, T.bh[:, d:d + 1], 0.0, A.subtract, A.min)]
        else:
            aff("k" + t, src + ["l_b"], xb, pick("kw", a, w), -1.0, T.bs[:, d:d + 1])
        if way == "z":
            op("z" + t, "g", ["k" + t, "l_q"], lambda e, xb=xb, qs=qs: e.dma_start(xb, qs, accum_op=A.add), kind="dma")
            clamped = [ts("r" + t, ["z" + t], rb, xb, 0.0, None, A.max)]
        if way == "p":
            nx = (nx + (nx % 2 if w == NC else 0)) % 4
            banks, px = range(nx, nx + w // 512), T["px%d" % (nx // 2)][:, 512 * (nx % 2):512 * (nx % 2) + w]

            def addq(e, nx=nx, lo=lo, a=a, w=w):
                for x in range(0, w, 512):
                    to = T["px%d" % (nx // 2)][:, 512 * (nx % 2) + x:512 * (nx % 2) + x + 512]
                    e.matmul(to, T.idb[:], T.qs[:, a + x:a + x + 512], True, False)
                    r = e.matmul(to, T.idb[:], T.xb[:, lo + x:lo + x + 512], False, True)
                return r
            op("a" + t, "p", ["k" + t, "l_q", "c_id"] + [xfree[u] for u in banks], addq)
            clamped = [aff("r" + t, ["a" + t], rb, px, func=F.Relu)]
            for u in banks:
                xfree[u] = clamped[0]
            nx = (nx + w // 512) % 4
        vsrc = [lists[d], "l_v"] + clamped + have["v", d]
        neg = int(way == "v")

        def times(name, a, w, d=d, pick=pick, vsrc=vsrc):
            x = NC * d + a
            return tt(name, vsrc, T.pb[:, x:x + w], pick("vw", a, w), T.rb[:, x:x + w], A.mult)
        if z < len(items) - 1:
            adds("c" + t, [times("p" + t, a, w)], d, a, w, neg)
        else:
            adds("c%s0" % t, [times("p%s0" % t, 512, 256)], d, 512, 256, neg)
            tt("y2", [times("p%s1" % t, 768, 256)] + acc[2], T.ys[:, 768:NC], T.plb[:, 0:256], T.pb[:, NC * d + 768:NC * d + NC],
               A.subtract if neg else A.add)
    for u, (bank, x, z) in enumerate(ACC):
        if u < 2:
            aff("y%d" % u, acc[u], T.ys[:, x:x + z], T[bank][:, 0:z])
        dma("st%d" % u, "sas"[u], ["y%d" % u], T.y[:, x:x + z], T.ys[:, x:x + z])
    return ops


def rank_program(g, core, T, topo):
    rank = T.rank_of(core)
    if rank is None:
        return
    n = len(T.cores)
    near = [T.cores[r] for r in (rank - 1, rank + 1) if 0 <= r < n]
    eng = [e for e in topo.engines(core, near[0]) if e in topo.engines(core, near[-1])]
    eng = eng[::len(eng) // 8]
    peers = {"all": sum(1 << e for e in eng), "half": [sum(1 << e for e in eng[0:4]), sum(1 << e for e in eng[4:8])]}
    if rank > 0:
        peers["prev"] = topo.addr(T.cores[rank - 1], core)
    if rank < n - 1:
        peers["next"] = topo.addr(T.cores[rank + 1], core)
    ops = {o["name"]: o for o in plan(T, rank, n, peers) if o["on"]}
    needed = {d for o in ops.values() for d in o["deps"]}
    queue = {"v": g.vector, "a": g.scalar, "p": g.tensor, "g": g, "s": g.sync}
    count = {"v": 0, "a": 0, "p": 0, "g": 0}
    mark, seen, sent = {}, {q: {} for q in queue}, 0
    order = ORDER.split()
    assert all(name in order for name in ops)
    for name in order:
        if name not in ops:
            continue
        o = ops[name]
        if o["kind"] == "arr":
            mark[name] = (name, len(eng))
            continue
        e = queue[o["eng"]]
        want = {}
        for d in o["deps"]:
            assert d in mark or d not in ops
            if d in mark and not (o["eng"] == "p" == ops[d]["eng"]):
                s, v = mark[d]
                want[s] = max(want.get(s, 0), v)
        for s, v in want.items():
            if seen[o["eng"]].get(s, 0) < v:
                e.wait_ge(T.sem[s], v)
                seen[o["eng"]][s] = v
        r = o["fn"](e)
        if o["kind"] == "dma":
            r.then_inc(T.sem[name], 16)
            mark[name] = (name, 16)
        elif o["kind"] == "rem":
            sent += len(eng)
        elif name in needed:
            count[o["eng"]] += 1
            r.then_inc(T.sem["c" + o["eng"]], 1)
            mark[name] = ("c" + o["eng"], count[o["eng"]])
    last = {}
    for s, v in mark.values():
        last[s] = max(last.get(s, 0), v)
    if sent:
        last["sent"] = sent
    for s, v in last.items():
        if max(seen[q].get(s, 0) for q in seen) < v:
            g.wait_ge(T.sem[s], v)
